import numpy as np
import ml_dtypes


def mxq(x, axis, fmt="e4m3"):
    dtype, down = {"e4m3": (ml_dtypes.float8_e4m3fn, 7), "e5m2": (ml_dtypes.float8_e5m2, 14)}[fmt]
    v = np.moveaxis(np.asarray(x, np.float32).astype(ml_dtypes.bfloat16).astype(np.float64), axis, -1)
    blocks = v.reshape(v.shape[:-1] + (-1, 32))
    amax = np.abs(blocks).max(-1, keepdims=True)
    byte = np.maximum(np.where(amax > 0, np.frexp(amax)[1] - 1 + 127, 0) - down, 1)
    scale = np.exp2(byte - 127.0)
    codes = (blocks / scale).astype(np.float32).astype(dtype).astype(np.float64)
    return np.moveaxis((codes * scale).reshape(v.shape), -1, axis)


WIDE = False


def mx_kscale(k):
    if not WIDE:
        return np.ones(k)
    levels = np.array([10, -10, 5, -5, 0])
    if k % 512:
        return np.exp2(np.random.permutation(np.resize(levels, k // 32))).repeat(32)
    a = np.empty((k // 512, 16))
    for p in range(k // 512):
        a[p, :8] = np.random.permutation(np.resize(levels, 8))
        for g in range(8):
            far = levels[np.abs(levels - a[p, g]) >= 10]
            a[p, g + 8] = far[np.random.randint(len(far))]
    return np.exp2(a.ravel()).repeat(32)


def f64(x):
    return np.asarray(x).astype(np.float64)


def striped8(idx):
    return np.concatenate([v.reshape(-1, 16).T for v in idx]).astype(np.uint16)


def unstriped8(offs):
    return np.stack([offs[16 * g:16 * g + 16].T.reshape(-1) for g in range(8)]).astype(np.int64)


E2M1 = np.array([0.0, 0.5, 1.0, 1.5, 2.0, 3.0, 4.0, 6.0, -0.0, -0.5, -1.0, -1.5, -2.0, -3.0, -4.0, -6.0])


def pack_weight(w, fmt):
    k, n = w.shape
    w = f64(np.asarray(w, np.float32).astype(ml_dtypes.bfloat16)).reshape(k // 32, 32, n)
    amax = np.abs(w).max(1)
    if fmt == "e4m3":
        byte = np.frexp(amax)[1] - 1 + 127 - 7
    else:
        mant, ex = np.frexp(amax / 6.0)
        byte = np.where(mant > 0.5, ex, ex - 1) + 127
    byte = np.clip(np.where(amax > 0, byte, 1), 1, 254)
    scaled = (w * np.exp2(127.0 - byte)[:, None, :]).reshape(k, n).astype(np.float32)
    by_word = np.ascontiguousarray(scaled.reshape(k // 512, 128, 4, n).transpose(0, 1, 3, 2))
    if fmt == "e4m3":
        words = by_word.astype(ml_dtypes.float8_e4m3fn).view(np.uint8)
    else:
        c = by_word.astype(ml_dtypes.float4_e2m1fn).view(np.uint8) & 0xF
        words = (c[..., 0::2] | (c[..., 1::2] << 4)).reshape(k // 512, 128, 2 * n)
    return np.ascontiguousarray(words), np.ascontiguousarray(byte.astype(np.uint8).reshape(k // 512, 16, n))


def unpack_weight(words, scales, fmt):
    g, _, n = scales.shape
    words = np.ascontiguousarray(words).reshape(g, 128, n, -1)
    if fmt == "e4m3":
        vals = words.view(ml_dtypes.float8_e4m3fn).astype(np.float64)
    else:
        nib = np.empty((g, 128, n, 4), np.uint8)
        nib[..., 0::2] = words & 0xF
        nib[..., 1::2] = words >> 4
        vals = E2M1[nib]
    vals = vals * np.repeat(np.exp2(scales.astype(np.float64) - 127.0), 8, axis=1)[..., None]
    return vals.transpose(0, 1, 3, 2).reshape(g * 512, n)


K, M, T, S = 1536, 512, 1024, 512


def setup_inputs():
    n = np.random.standard_normal
    s = mx_kscale(K)[:, None]
    w = n((K, M)) / np.sqrt(K) / s
    w4 = pack_weight(w, "e2m1")
    rest = w - unpack_weight(*w4, "e2m1")
    p_r8 = pack_weight(rest, "e4m3")
    return {
        "xT": (n((K, T)) * s).astype(np.float32),
        "w4_words": w4[0],
        "w4_scales": w4[1],
        "r8_words": p_r8[0],
        "r8_scales": p_r8[1],
        "wgt": np.repeat(np.random.uniform(0.5, 2.0, (8, S)), 16, axis=0).astype(np.float32),
        "b": (0.3 * n(512)).astype(np.float32),
        "wgo": np.repeat(np.random.uniform(0.5, 2.0, (8, S)), 16, axis=0).astype(np.float32),
        "offs": striped8(np.stack([np.random.permutation(T)[:S] for _ in range(8)])),
        "offs2": striped8(np.stack([np.random.permutation(T)[:S] for _ in range(8)])),
    }


def reference(xT, w4_words, w4_scales, r8_words, r8_scales, wgt, b, wgo, offs, offs2):
    idx = unstriped8(offs)
    group = np.arange(K) % 512 // 64
    xg = f64(wgt)[np.arange(K) // 4 % 128] * f64(xT)[np.arange(K)[:, None], idx[group]]
    xT_ = mxq(xg, 0, "e4m3")
    w4_ = unpack_weight(w4_words, w4_scales, "e2m1")
    r8_ = unpack_weight(r8_words, r8_scales, "e4m3")
    y = w4_.T @ xT_ + r8_.T @ xT_
    place = unstriped8(offs2)[np.arange(M) % 128 // 16]
    out = np.zeros((M, T))
    out[np.arange(M)[:, None], place] = f64(wgo)[np.arange(M) % 128] * (y + f64(b)[:, None])
    return out

@@ -1,0 +1,173 @@
+from contextlib import ExitStack
+
+import concourse.mybir as mybir
+
+K, M, T, S = 1536, 512, 1024, 512
+FLOPS = 2 * 2 * K * M * S
+
+F32 = mybir.dt.float32
+BF16 = mybir.dt.bfloat16
+I32 = mybir.dt.int32
+U32 = mybir.dt.uint32
+U16 = mybir.dt.uint16
+U8 = mybir.dt.uint8
+E4M3 = mybir.dt.float8_e4m3fn_x4
+E2M1 = mybir.dt.float4_e2m1fn_x4
+MULT = mybir.AluOpType.mult
+IDENTITY = mybir.ActivationFunctionType.Identity
+
+P = 128
+PACK = 4
+PASSES = K // (P * PACK)
+M_TILES = M // P
+HALVES = 2
+H = S // HALVES
+HC = H // 16
+N = 128
+Q = H // N
+
+
+def tile_list_hboth_bias_kernel(
+    tc, xT, w4_words, w4_scales, r8_words, r8_scales, wgt, b, wgo, offs, offs2, out
+):
+    nc = tc.nc
+    with ExitStack() as ctx:
+        keep = ctx.enter_context(tc.tile_pool(name="keep", bufs=1))
+        psum = ctx.enter_context(tc.psum_pool(name="psum", bufs=1))
+
+        offs_t = keep.tile([P, S // 16], U16, name="offs_t")
+        offs2_t = keep.tile([P, S // 16], U16, name="offs2_t")
+        wgt_t = [keep.tile([P, H], F32, name=f"wgt{h}") for h in range(HALVES)]
+        wgo_t = keep.tile([P, S], F32, name="wgo_t")
+        b_t = keep.tile([P, M_TILES], F32, name="b_t")
+        x_t = [[keep.tile([P, T], F32, name=f"x{a}_{j}") for j in range(PACK)] for a in range(PASSES)]
+        w4_t = keep.tile([P, PASSES, 2 * M], U8, name="w4_t", align_bytes=64)
+        r8_t = keep.tile([P, PASSES, 4 * M], U8, name="r8_t", align_bytes=64)
+        w4_s = keep.tile([P, PASSES, M], U8, name="w4_s", align_bytes=64)
+        r8_s = keep.tile([P, PASSES, M], U8, name="r8_s", align_bytes=64)
+        win = [keep.tile([P, T], F32, name=f"win{m}") for m in range(M_TILES)]
+
+        x_v = xT.rearrange("(a p j) t -> a j p t", p=P, j=PACK)
+        nc.sync.dma_start(offs_t[:], offs)
+        nc.sync.dma_start(wgt_t[0][:], wgt[:, 0:H])
+        nc.sync.dma_start(x_t[0][0][:], x_v[0, 0])
+        nc.sync.dma_start(x_t[0][1][:], x_v[0, 1])
+        nc.sync.dma_start(wgt_t[1][:], wgt[:, H:S])
+        nc.sync.dma_start(x_t[0][2][:], x_v[0, 2])
+        nc.sync.dma_start(x_t[0][3][:], x_v[0, 3])
+        for j in range(PACK):
+            nc.sync.dma_start(x_t[1][j][:], x_v[1, j])
+        for j in range(PACK):
+            nc.sync.dma_start(x_t[2][j][:], x_v[2, j])
+        r8_v = r8_words.rearrange("a p n i -> p a (n i)")
+        w4_v = w4_words.rearrange("a p n -> p a n")
+        for half in range(2):
+            cols = slice(half * 2 * M, (half + 1) * 2 * M)
+            nc.sync.dma_start(r8_t[:, :, cols].bitcast(I32), r8_v[:, :, cols].bitcast(I32))
+            cols = slice(half * M, (half + 1) * M)
+            nc.sync.dma_start(w4_t[:, :, cols].bitcast(I32), w4_v[:, :, cols].bitcast(I32))
+        nc.sync.dma_start(offs2_t[:], offs2)
+        nc.sync.dma_start(wgo_t[:], wgo)
+
+        nc.gpsimd.memset(r8_s[:].bitcast(I32), 0)
+        nc.gpsimd.memset(w4_s[:].bitcast(I32), 0)
+        for tile_s, scales in ((r8_s, r8_scales), (w4_s, w4_scales)):
+            for q in range(4):
+                nc.gpsimd.dma_start(
+                    tile_s[32 * q : 32 * q + 4, :, :].bitcast(I32),
+                    scales[:, 4 * q : 4 * q + 4, :].rearrange("a q n -> q a n").bitcast(I32),
+                )
+        nc.gpsimd.dma_start(b_t[:], b.rearrange("(m p) -> p m", p=P))
+
+        for m in range(M_TILES):
+            nc.vector.memset(win[m][:], 0.0)
+
+        codes = {}
+        scales_x = {}
+
+        def select(a, h):
+            cols = slice(h * HC, (h + 1) * HC)
+            g = keep.tile([P, PACK, H], F32, name=f"g{a}_{h}")
+            for j in range(PACK):
+                nc.vector.tensor_tensor(
+                    g[:, j, :], x_t[a][j][:].indirect(offs_t[:, cols]), wgt_t[h][:], MULT
+                )
+            packed = keep.tile([P, H, PACK], BF16, name=f"packed{a}_{h}", align_bytes=64)
+            nc.scalar.copy(out=packed[:], in_=g[:].rearrange("p j w -> p w j"))
+            c = keep.tile([P, H], U32, name=f"codes{a}_{h}", align_bytes=64)
+            s = keep.tile([P, H], U8, name=f"scales{a}_{h}", align_bytes=64)
+            nc.vector.quantize_mx(
+                out=c[:].bitcast(E4M3), scales=s[:], in_=packed[:].rearrange("p w j -> p (w j)")
+            )
+            codes[a, h] = c
+            scales_x[a, h] = s
+
+        def multiply(acc, a, h, m, q):
+            n_cols = slice(q * N, (q + 1) * N)
+            rhs = codes[a, h][:, n_cols].bitcast(E4M3)
+            rhs_scale = scales_x[a, h][:, n_cols]
+            nc.tensor.matmul_mx(
+                out=acc[:],
+                lhsT=r8_t[:, a, m * 4 * P : (m + 1) * 4 * P].bitcast(E4M3),
+                lhsT_scale=r8_s[:, a, m * P : (m + 1) * P],
+                rhs=rhs,
+                rhs_scale=rhs_scale,
+                start=(a == 0),
+                stop=False,
+            )
+            nc.tensor.matmul_mx(
+                out=acc[:],
+                lhsT=w4_t[:, a, m * 2 * P : (m + 1) * 2 * P].bitcast(E2M1),
+                lhsT_scale=w4_s[:, a, m * P : (m + 1) * P],
+                rhs=rhs,
+                rhs_scale=rhs_scale,
+                start=False,
+                stop=(a == PASSES - 1),
+            )
+
+        accs = {}
+        y = {}
+
+        def open_bank(h, m, q):
+            acc = psum.tile([P, N], F32, name=f"acc{m}_{q}")
+            accs[h, m, q] = acc
+            return acc
+
+        def empty_bank(h, m, q):
+            nc.scalar.activation(
+                y[h, m][:, q * N : (q + 1) * N], accs[h, m, q][:], IDENTITY, bias=b_t[:, m : m + 1]
+            )
+
+        def scatter(h, m):
+            cols = slice(h * HC, (h + 1) * HC)
+            nc.vector.tensor_tensor(
+                win[m][:].indirect(offs2_t[:, cols]), y[h, m][:], wgo_t[:, h * H : (h + 1) * H], MULT
+            )
+
+        for h in range(HALVES):
+            for m in range(M_TILES):
+                y[h, m] = keep.tile([P, H], F32, name=f"y{h}_{m}")
+
+        for m in range(M_TILES):
+            for q in range(Q):
+                open_bank(0, m, q)
+        for a in range(PASSES):
+            select(a, 0)
+        for m in range(M_TILES):
+            for a in range(PASSES):
+                for q in range(Q):
+                    multiply(accs[0, m, q], a, 0, m, q)
+            for q in range(Q):
+                empty_bank(0, m, q)
+        for a in range(PASSES):
+            select(a, 1)
+        for m in range(M_TILES):
+            scatter(0, m)
+        for m in range(M_TILES):
+            for q in range(Q):
+                acc = open_bank(1, m, q)
+                for a in range(PASSES):
+                    multiply(acc, a, 1, m, q)
+                empty_bank(1, m, q)
+            scatter(1, m)
+            nc.sync.dma_start(out[m * P : (m + 1) * P, :], win[m][:])

@@ -1,6 +1,7 @@
 from contextlib import ExitStack
 
 import concourse.mybir as mybir
+from concourse.masks import make_identity
 
 K, M, T, S = 1536, 512, 1024, 512
 FLOPS = 2 * 2 * K * M * S
@@ -39,6 +40,8 @@ def tile_list_hboth_bias_kernel(
         offs2_t = keep.tile([P, S // 16], U16, name="offs2_t")
         wgt_t = [keep.tile([P, H], F32, name=f"wgt{h}") for h in range(HALVES)]
         wgo_t = keep.tile([P, S], F32, name="wgo_t")
+        b_rows = keep.tile([P, P], F32, name="b_rows")
+        ident = keep.tile([P, P], F32, name="ident")
         b_t = keep.tile([P, M_TILES], F32, name="b_t")
         x_t = [[keep.tile([P, T], F32, name=f"x{a}_{j}") for j in range(PACK)] for a in range(PASSES)]
         w4_t = keep.tile([P, PASSES, 2 * M], U8, name="w4_t", align_bytes=64)
@@ -48,17 +51,15 @@ def tile_list_hboth_bias_kernel(
         win = [keep.tile([P, T], F32, name=f"win{m}") for m in range(M_TILES)]
 
         x_v = xT.rearrange("(a p j) t -> a j p t", p=P, j=PACK)
+        nc.sync.dma_start(x_t[0][0][:], x_v[0, 0])
         nc.sync.dma_start(offs_t[:], offs)
         nc.sync.dma_start(wgt_t[0][:], wgt[:, 0:H])
-        nc.sync.dma_start(x_t[0][0][:], x_v[0, 0])
         nc.sync.dma_start(x_t[0][1][:], x_v[0, 1])
         nc.sync.dma_start(wgt_t[1][:], wgt[:, H:S])
-        nc.sync.dma_start(x_t[0][2][:], x_v[0, 2])
-        nc.sync.dma_start(x_t[0][3][:], x_v[0, 3])
-        for j in range(PACK):
-            nc.sync.dma_start(x_t[1][j][:], x_v[1, j])
-        for j in range(PACK):
-            nc.sync.dma_start(x_t[2][j][:], x_v[2, j])
+        for a in range(PASSES):
+            for j in range(PACK):
+                if (a, j) not in ((0, 0), (0, 1)):
+                    nc.sync.dma_start(x_t[a][j][:], x_v[a, j])
         r8_v = r8_words.rearrange("a p n i -> p a (n i)")
         w4_v = w4_words.rearrange("a p n -> p a n")
         for half in range(2):
@@ -66,52 +67,69 @@ def tile_list_hboth_bias_kernel(
             nc.sync.dma_start(r8_t[:, :, cols].bitcast(I32), r8_v[:, :, cols].bitcast(I32))
             cols = slice(half * M, (half + 1) * M)
             nc.sync.dma_start(w4_t[:, :, cols].bitcast(I32), w4_v[:, :, cols].bitcast(I32))
-        nc.sync.dma_start(offs2_t[:], offs2)
-        nc.sync.dma_start(wgo_t[:], wgo)
+            if half == 0:
+                nc.sync.dma_start(offs2_t[:], offs2)
+                nc.sync.dma_start(wgo_t[:], wgo)
 
         nc.gpsimd.memset(r8_s[:].bitcast(I32), 0)
         nc.gpsimd.memset(w4_s[:].bitcast(I32), 0)
+        nc.gpsimd.memset(b_rows[:], 0.0)
+        make_identity(nc, ident[:])
+        nc.gpsimd.dma_start(b_rows[0:M_TILES, :], b.rearrange("(m p) -> m p", p=P))
         for tile_s, scales in ((r8_s, r8_scales), (w4_s, w4_scales)):
             for q in range(4):
                 nc.gpsimd.dma_start(
                     tile_s[32 * q : 32 * q + 4, :, :].bitcast(I32),
                     scales[:, 4 * q : 4 * q + 4, :].rearrange("a q n -> q a n").bitcast(I32),
                 )
-        nc.gpsimd.dma_start(b_t[:], b.rearrange("(m p) -> p m", p=P))
+        b_cols = psum.tile([P, P], F32, name="acc1_1_1")
+        nc.tensor.transpose(b_cols[:], b_rows[:], ident[:])
+        nc.scalar.copy(out=b_t[:], in_=b_cols[:, 0:M_TILES])
 
         for m in range(M_TILES):
             nc.vector.memset(win[m][:], 0.0)
 
-        codes = {}
-        scales_x = {}
+        def gather(dst, a, j, h):
+            nc.vector.tensor_tensor(
+                dst, x_t[a][j][:].indirect(offs_t[:, h * HC : (h + 1) * HC]), wgt_t[h][:], MULT
+            )
 
-        def select(a, h):
-            cols = slice(h * HC, (h + 1) * HC)
-            g = keep.tile([P, PACK, H], F32, name=f"g{a}_{h}")
-            for j in range(PACK):
-                nc.vector.tensor_tensor(
-                    g[:, j, :], x_t[a][j][:].indirect(offs_t[:, cols]), wgt_t[h][:], MULT
-                )
-            packed = keep.tile([P, H, PACK], BF16, name=f"packed{a}_{h}", align_bytes=64)
-            nc.scalar.copy(out=packed[:], in_=g[:].rearrange("p j w -> p w j"))
-            c = keep.tile([P, H], U32, name=f"codes{a}_{h}", align_bytes=64)
-            s = keep.tile([P, H], U8, name=f"scales{a}_{h}", align_bytes=64)
+        def interleave(g, width, name):
+            packed = keep.tile([P, width, PACK], BF16, name=f"packed{name}", align_bytes=64)
+            nc.scalar.copy(
+                out=packed[:].rearrange("p (c i) j -> p c j i", i=4),
+                in_=g[:].rearrange("p j (c i) -> p c j i", i=4),
+            )
+            return packed
+
+        def quantise(packed, width, name):
+            c = keep.tile([P, width], U32, name=f"codes{name}", align_bytes=64)
+            s = keep.tile([P, width], U8, name=f"scales{name}", align_bytes=64)
             nc.vector.quantize_mx(
                 out=c[:].bitcast(E4M3), scales=s[:], in_=packed[:].rearrange("p w j -> p (w j)")
             )
-            codes[a, h] = c
-            scales_x[a, h] = s
+            return c, s
+
+        rhs = {}
+
+        def select(a, h):
+            g = keep.tile([P, PACK, H], F32, name=f"g{a}_{h}")
+            for j in range(PACK):
+                gather(g[:, j, :], a, j, h)
+            rhs[a, h] = quantise(interleave(g, H, f"{a}_{h}"), H, f"{a}_{h}")
+
+        for a in range(PASSES):
+            select(a, 0)
 
         def multiply(acc, a, h, m, q):
+            c, s = rhs[a, h]
             n_cols = slice(q * N, (q + 1) * N)
-            rhs = codes[a, h][:, n_cols].bitcast(E4M3)
-            rhs_scale = scales_x[a, h][:, n_cols]
             nc.tensor.matmul_mx(
                 out=acc[:],
                 lhsT=r8_t[:, a, m * 4 * P : (m + 1) * 4 * P].bitcast(E4M3),
                 lhsT_scale=r8_s[:, a, m * P : (m + 1) * P],
-                rhs=rhs,
-                rhs_scale=rhs_scale,
+                rhs=c[:, n_cols].bitcast(E4M3),
+                rhs_scale=s[:, n_cols],
                 start=(a == 0),
                 stop=False,
             )
@@ -119,23 +137,17 @@ def tile_list_hboth_bias_kernel(
                 out=acc[:],
                 lhsT=w4_t[:, a, m * 2 * P : (m + 1) * 2 * P].bitcast(E2M1),
                 lhsT_scale=w4_s[:, a, m * P : (m + 1) * P],
-                rhs=rhs,
-                rhs_scale=rhs_scale,
+                rhs=c[:, n_cols].bitcast(E4M3),
+                rhs_scale=s[:, n_cols],
                 start=False,
                 stop=(a == PASSES - 1),
             )
 
-        accs = {}
         y = {}
 
-        def open_bank(h, m, q):
-            acc = psum.tile([P, N], F32, name=f"acc{m}_{q}")
-            accs[h, m, q] = acc
-            return acc
-
-        def empty_bank(h, m, q):
+        def empty_bank(h, m, q, acc):
             nc.scalar.activation(
-                y[h, m][:, q * N : (q + 1) * N], accs[h, m, q][:], IDENTITY, bias=b_t[:, m : m + 1]
+                y[h, m][:, q * N : (q + 1) * N], acc[:], IDENTITY, bias=b_t[:, m : m + 1]
             )
 
         def scatter(h, m):
@@ -148,26 +160,21 @@ def tile_list_hboth_bias_kernel(
             for m in range(M_TILES):
                 y[h, m] = keep.tile([P, H], F32, name=f"y{h}_{m}")
 
-        for m in range(M_TILES):
-            for q in range(Q):
-                open_bank(0, m, q)
-        for a in range(PASSES):
-            select(a, 0)
-        for m in range(M_TILES):
+        def product(h, m):
+            accs = [psum.tile([P, N], F32, name=f"acc{h}_{m % 2}_{q}") for q in range(Q)]
             for a in range(PASSES):
                 for q in range(Q):
-                    multiply(accs[0, m, q], a, 0, m, q)
+                    multiply(accs[q], a, h, m, q)
             for q in range(Q):
-                empty_bank(0, m, q)
+                empty_bank(h, m, q, accs[q])
+
+        for m in range(M_TILES):
+            product(0, m)
         for a in range(PASSES):
             select(a, 1)
         for m in range(M_TILES):
             scatter(0, m)
         for m in range(M_TILES):
-            for q in range(Q):
-                acc = open_bank(1, m, q)
-                for a in range(PASSES):
-                    multiply(acc, a, 1, m, q)
-                empty_bank(1, m, q)
+            product(1, m)
             scatter(1, m)
             nc.sync.dma_start(out[m * P : (m + 1) * P, :], win[m][:])

@@ -20,6 +20,7 @@ IDENTITY = mybir.ActivationFunctionType.Identity
 P = 128
 PACK = 4
 PASSES = K // (P * PACK)
+PLANES = PASSES * PACK
 M_TILES = M // P
 HALVES = 2
 H = S // HALVES
@@ -43,23 +44,20 @@ def tile_list_hboth_bias_kernel(
         b_rows = keep.tile([P, P], F32, name="b_rows")
         ident = keep.tile([P, P], F32, name="ident")
         b_t = keep.tile([P, M_TILES], F32, name="b_t")
-        x_t = [[keep.tile([P, T], F32, name=f"x{a}_{j}") for j in range(PACK)] for a in range(PASSES)]
+        x_t = [keep.tile([P, T], F32, name=f"x{i}") for i in range(PLANES)]
         w4_t = keep.tile([P, PASSES, 2 * M], U8, name="w4_t", align_bytes=64)
         r8_t = keep.tile([P, PASSES, 4 * M], U8, name="r8_t", align_bytes=64)
         w4_s = keep.tile([P, PASSES, M], U8, name="w4_s", align_bytes=64)
         r8_s = keep.tile([P, PASSES, M], U8, name="r8_s", align_bytes=64)
         win = [keep.tile([P, T], F32, name=f"win{m}") for m in range(M_TILES)]
 
-        x_v = xT.rearrange("(a p j) t -> a j p t", p=P, j=PACK)
-        nc.sync.dma_start(x_t[0][0][:], x_v[0, 0])
+        x_v = [xT.rearrange("(a p j) t -> a j p t", p=P, j=PACK)[i // PACK, i % PACK] for i in range(PLANES)]
+        nc.sync.dma_start(x_t[0][:], x_v[0])
         nc.sync.dma_start(offs_t[:], offs)
-        nc.sync.dma_start(wgt_t[0][:], wgt[:, 0:H])
-        nc.sync.dma_start(x_t[0][1][:], x_v[0, 1])
-        nc.sync.dma_start(wgt_t[1][:], wgt[:, H:S])
-        for a in range(PASSES):
-            for j in range(PACK):
-                if (a, j) not in ((0, 0), (0, 1)):
-                    nc.sync.dma_start(x_t[a][j][:], x_v[a, j])
+        for h in range(HALVES):
+            nc.sync.dma_start(wgt_t[h][:], wgt[:, h * H : (h + 1) * H])
+        for p in range(1, PLANES):
+            nc.sync.dma_start(x_t[p][:], x_v[p])
         r8_v = r8_words.rearrange("a p n i -> p a (n i)")
         w4_v = w4_words.rearrange("a p n -> p a n")
         for half in range(2):
@@ -89,37 +87,38 @@ def tile_list_hboth_bias_kernel(
         for m in range(M_TILES):
             nc.vector.memset(win[m][:], 0.0)
 
-        def gather(dst, a, j, h):
-            nc.vector.tensor_tensor(
-                dst, x_t[a][j][:].indirect(offs_t[:, h * HC : (h + 1) * HC]), wgt_t[h][:], MULT
-            )
-
-        def interleave(g, width, name):
-            packed = keep.tile([P, width, PACK], BF16, name=f"packed{name}", align_bytes=64)
-            nc.scalar.copy(
-                out=packed[:].rearrange("p (c i) j -> p c j i", i=4),
-                in_=g[:].rearrange("p j (c i) -> p c j i", i=4),
-            )
-            return packed
-
-        def quantise(packed, width, name):
-            c = keep.tile([P, width], U32, name=f"codes{name}", align_bytes=64)
-            s = keep.tile([P, width], U8, name=f"scales{name}", align_bytes=64)
-            nc.vector.quantize_mx(
-                out=c[:].bitcast(E4M3), scales=s[:], in_=packed[:].rearrange("p w j -> p (w j)")
-            )
-            return c, s
-
+        g_t = {}
+        packed = {}
         rhs = {}
+        for h in range(HALVES):
+            for a in range(PASSES):
+                g_t[a, h] = keep.tile([P, PACK, H], F32, name=f"g{a}_{h}")
+                packed[a, h] = keep.tile([P, H, PACK], BF16, name=f"packed{a}_{h}", align_bytes=64)
+                c = keep.tile([P, H], U32, name=f"codes{a}_{h}", align_bytes=64)
+                s = keep.tile([P, H], U8, name=f"scales{a}_{h}", align_bytes=64)
+                rhs[a, h] = (c, s)
 
-        def select(a, h):
-            g = keep.tile([P, PACK, H], F32, name=f"g{a}_{h}")
-            for j in range(PACK):
-                gather(g[:, j, :], a, j, h)
-            rhs[a, h] = quantise(interleave(g, H, f"{a}_{h}"), H, f"{a}_{h}")
+        def gather(i, h):
+            nc.vector.tensor_tensor(
+                g_t[i // PACK, h][:, i % PACK, :],
+                x_t[i][:].indirect(offs_t[:, h * HC : (h + 1) * HC]),
+                wgt_t[h][:],
+                MULT,
+            )
 
-        for a in range(PASSES):
-            select(a, 0)
+        def interleave(a, h):
+            nc.scalar.copy(
+                out=packed[a, h][:].rearrange("p (c i) j -> p c j i", i=4),
+                in_=g_t[a, h][:].rearrange("p j (c i) -> p c j i", i=4),
+            )
+
+        def quantise(a, h):
+            c, s = rhs[a, h]
+            nc.vector.quantize_mx(
+                out=c[:].bitcast(E4M3),
+                scales=s[:],
+                in_=packed[a, h][:].rearrange("p w j -> p (w j)"),
+            )
 
         def multiply(acc, a, h, m, q):
             c, s = rhs[a, h]
@@ -168,12 +167,34 @@ def tile_list_hboth_bias_kernel(
             for q in range(Q):
                 empty_bank(h, m, q, accs[q])
 
+        for a in range(PASSES - 1):
+            for j in range(PACK):
+                for h in range(HALVES):
+                    gather(a * PACK + j, h)
+            for h in range(HALVES):
+                interleave(a, h)
+        gather(8, 0)
+        gather(9, 0)
+        gather(8, 1)
+        gather(10, 0)
+        gather(11, 0)
+        interleave(2, 0)
+        quantise(0, 0)
+        quantise(1, 0)
+        quantise(0, 1)
+        gather(9, 1)
+        quantise(2, 0)
+        gather(10, 1)
+        quantise(1, 1)
+        gather(11, 1)
         for m in range(M_TILES):
             product(0, m)
-        for a in range(PASSES):
-            select(a, 1)
-        for m in range(M_TILES):
-            scatter(0, m)
+        interleave(2, 1)
+        scatter(0, 0)
+        scatter(0, 1)
+        quantise(2, 1)
+        scatter(0, 2)
+        scatter(0, 3)
         for m in range(M_TILES):
             product(1, m)
             scatter(1, m)

from contextlib import ExitStack

import concourse.mybir as mybir
from concourse.masks import make_identity

K, M, T, S = 1536, 512, 1024, 512
FLOPS = 2 * 2 * K * M * S

F32 = mybir.dt.float32
BF16 = mybir.dt.bfloat16
I32 = mybir.dt.int32
U32 = mybir.dt.uint32
U16 = mybir.dt.uint16
U8 = mybir.dt.uint8
E4M3 = mybir.dt.float8_e4m3fn_x4
E2M1 = mybir.dt.float4_e2m1fn_x4
MULT = mybir.AluOpType.mult
IDENTITY = mybir.ActivationFunctionType.Identity

P = 128
PACK = 4
PASSES = K // (P * PACK)
PLANES = PASSES * PACK
M_TILES = M // P
HALVES = 2
H = S // HALVES
HC = H // 16
N = 128
Q = H // N


def tile_list_hboth_bias_kernel(
    tc, xT, w4_words, w4_scales, r8_words, r8_scales, wgt, b, wgo, offs, offs2, out
):
    nc = tc.nc
    with ExitStack() as ctx:
        keep = ctx.enter_context(tc.tile_pool(name="keep", bufs=1))
        psum = ctx.enter_context(tc.psum_pool(name="psum", bufs=1))

        offs_t = keep.tile([P, S // 16], U16, name="offs_t")
        offs2_t = keep.tile([P, S // 16], U16, name="offs2_t")
        wgt_t = [keep.tile([P, H], F32, name=f"wgt{h}") for h in range(HALVES)]
        wgo_t = keep.tile([P, S], F32, name="wgo_t")
        b_rows = keep.tile([P, P], F32, name="b_rows")
        ident = keep.tile([P, P], F32, name="ident")
        b_t = keep.tile([P, M_TILES], F32, name="b_t")
        x_t = [keep.tile([P, T], F32, name=f"x{i}") for i in range(PLANES)]
        w4_t = keep.tile([P, PASSES, 2 * M], U8, name="w4_t", align_bytes=64)
        r8_t = keep.tile([P, PASSES, 4 * M], U8, name="r8_t", align_bytes=64)
        w4_s = keep.tile([P, PASSES, M], U8, name="w4_s", align_bytes=64)
        r8_s = keep.tile([P, PASSES, M], U8, name="r8_s", align_bytes=64)
        win = [keep.tile([P, T], F32, name=f"win{m}") for m in range(M_TILES)]

        x_v = [xT.rearrange("(a p j) t -> a j p t", p=P, j=PACK)[i // PACK, i % PACK] for i in range(PLANES)]
        nc.sync.dma_start(x_t[0][:], x_v[0])
        nc.sync.dma_start(offs_t[:], offs)
        for h in range(HALVES):
            nc.sync.dma_start(wgt_t[h][:], wgt[:, h * H : (h + 1) * H])
        for p in range(1, PLANES):
            nc.sync.dma_start(x_t[p][:], x_v[p])
        r8_v = r8_words.rearrange("a p n i -> p a (n i)")
        w4_v = w4_words.rearrange("a p n -> p a n")
        for half in range(2):
            cols = slice(half * 2 * M, (half + 1) * 2 * M)
            nc.sync.dma_start(r8_t[:, :, cols].bitcast(I32), r8_v[:, :, cols].bitcast(I32))
            cols = slice(half * M, (half + 1) * M)
            nc.sync.dma_start(w4_t[:, :, cols].bitcast(I32), w4_v[:, :, cols].bitcast(I32))
            if half == 0:
                nc.sync.dma_start(offs2_t[:], offs2)
                nc.sync.dma_start(wgo_t[:], wgo)

        nc.gpsimd.memset(r8_s[:].bitcast(I32), 0)
        nc.gpsimd.memset(w4_s[:].bitcast(I32), 0)
        nc.gpsimd.memset(b_rows[:], 0.0)
        make_identity(nc, ident[:])
        nc.gpsimd.dma_start(b_rows[0:M_TILES, :], b.rearrange("(m p) -> m p", p=P))
        for tile_s, scales in ((r8_s, r8_scales), (w4_s, w4_scales)):
            for q in range(4):
                nc.gpsimd.dma_start(
                    tile_s[32 * q : 32 * q + 4, :, :].bitcast(I32),
                    scales[:, 4 * q : 4 * q + 4, :].rearrange("a q n -> q a n").bitcast(I32),
                )
        b_cols = psum.tile([P, P], F32, name="acc1_1_1")
        nc.tensor.transpose(b_cols[:], b_rows[:], ident[:])
        nc.scalar.copy(out=b_t[:], in_=b_cols[:, 0:M_TILES])

        for m in range(M_TILES):
            nc.vector.memset(win[m][:], 0.0)

        g_t = {}
        packed = {}
        rhs = {}
        for h in range(HALVES):
            for a in range(PASSES):
                g_t[a, h] = keep.tile([P, PACK, H], F32, name=f"g{a}_{h}")
                packed[a, h] = keep.tile([P, H, PACK], BF16, name=f"packed{a}_{h}", align_bytes=64)
                c = keep.tile([P, H], U32, name=f"codes{a}_{h}", align_bytes=64)
                s = keep.tile([P, H], U8, name=f"scales{a}_{h}", align_bytes=64)
                rhs[a, h] = (c, s)

        def gather(i, h):
            nc.vector.tensor_tensor(
                g_t[i // PACK, h][:, i % PACK, :],
                x_t[i][:].indirect(offs_t[:, h * HC : (h + 1) * HC]),
                wgt_t[h][:],
                MULT,
            )

        def interleave(a, h):
            nc.scalar.copy(
                out=packed[a, h][:].rearrange("p (c i) j -> p c j i", i=4),
                in_=g_t[a, h][:].rearrange("p j (c i) -> p c j i", i=4),
            )

        def quantise(a, h):
            c, s = rhs[a, h]
            nc.vector.quantize_mx(
                out=c[:].bitcast(E4M3),
                scales=s[:],
                in_=packed[a, h][:].rearrange("p w j -> p (w j)"),
            )

        def multiply(acc, a, h, m, q):
            c, s = rhs[a, h]
            n_cols = slice(q * N, (q + 1) * N)
            nc.tensor.matmul_mx(
                out=acc[:],
                lhsT=r8_t[:, a, m * 4 * P : (m + 1) * 4 * P].bitcast(E4M3),
                lhsT_scale=r8_s[:, a, m * P : (m + 1) * P],
                rhs=c[:, n_cols].bitcast(E4M3),
                rhs_scale=s[:, n_cols],
                start=(a == 0),
                stop=False,
            )
            nc.tensor.matmul_mx(
                out=acc[:],
                lhsT=w4_t[:, a, m * 2 * P : (m + 1) * 2 * P].bitcast(E2M1),
                lhsT_scale=w4_s[:, a, m * P : (m + 1) * P],
                rhs=c[:, n_cols].bitcast(E4M3),
                rhs_scale=s[:, n_cols],
                start=False,
                stop=(a == PASSES - 1),
            )

        y = {}

        def empty_bank(h, m, q, acc):
            nc.scalar.activation(
                y[h, m][:, q * N : (q + 1) * N], acc[:], IDENTITY, bias=b_t[:, m : m + 1]
            )

        def scatter(h, m):
            cols = slice(h * HC, (h + 1) * HC)
            nc.vector.tensor_tensor(
                win[m][:].indirect(offs2_t[:, cols]), y[h, m][:], wgo_t[:, h * H : (h + 1) * H], MULT
            )

        for h in range(HALVES):
            for m in range(M_TILES):
                y[h, m] = keep.tile([P, H], F32, name=f"y{h}_{m}")

        def product(h, m):
            accs = [psum.tile([P, N], F32, name=f"acc{h}_{m % 2}_{q}") for q in range(Q)]
            for a in range(PASSES):
                for q in range(Q):
                    multiply(accs[q], a, h, m, q)
            for q in range(Q):
                empty_bank(h, m, q, accs[q])

        for a in range(PASSES - 1):
            for j in range(PACK):
                for h in range(HALVES):
                    gather(a * PACK + j, h)
            for h in range(HALVES):
                interleave(a, h)
        gather(8, 0)
        gather(9, 0)
        gather(8, 1)
        gather(10, 0)
        gather(11, 0)
        interleave(2, 0)
        quantise(0, 0)
        quantise(1, 0)
        quantise(0, 1)
        gather(9, 1)
        quantise(2, 0)
        gather(10, 1)
        quantise(1, 1)
        gather(11, 1)
        for m in range(M_TILES):
            product(0, m)
        interleave(2, 1)
        scatter(0, 0)
        scatter(0, 1)
        quantise(2, 1)
        scatter(0, 2)
        scatter(0, 3)
        for m in range(M_TILES):
            product(1, m)
            scatter(1, m)
            nc.sync.dma_start(out[m * P : (m + 1) * P, :], win[m][:])
